import numpy as np
import ml_dtypes


def mxq(x, axis, fmt="e4m3"):
    dtype, down = {"e4m3": (ml_dtypes.float8_e4m3fn, 7), "e5m2": (ml_dtypes.float8_e5m2, 14)}[fmt]
    v = np.moveaxis(np.asarray(x, np.float32).astype(ml_dtypes.bfloat16).astype(np.float64), axis, -1)
    blocks = v.reshape(v.shape[:-1] + (-1, 32))
    amax = np.abs(blocks).max(-1, keepdims=True)
    byte = np.maximum(np.where(amax > 0, np.frexp(amax)[1] - 1 + 127, 0) - down, 1)
    scale = np.exp2(byte - 127.0)
    codes = (blocks / scale).astype(np.float32).astype(dtype).astype(np.float64)
    return np.moveaxis((codes * scale).reshape(v.shape), -1, axis)


WIDE = False


def mx_kscale(k):
    if not WIDE:
        return np.ones(k)
    levels = np.array([30, -30])
    if k % 512:
        return np.exp2(np.random.permutation(np.resize(levels, k // 32))).repeat(32)
    a = np.empty((k // 512, 16))
    for p in range(k // 512):
        a[p, :8] = np.random.permutation(np.resize(levels, 8))
        for g in range(8):
            far = levels[np.abs(levels - a[p, g]) >= 10]
            a[p, g + 8] = far[np.random.randint(len(far))]
    return np.exp2(a.ravel()).repeat(32)


def f64(x):
    return np.asarray(x).astype(np.float64)


def striped(idx):
    return np.tile(np.asarray(idx).reshape(-1, 16).T, (8, 1)).astype(np.uint16)


def unstriped(offs):
    return offs[:16].T.reshape(-1).astype(np.int64)


def striped8(idx):
    return np.asarray(idx).reshape(8, -1, 16).transpose(0, 2, 1).reshape(128, -1).astype(np.uint16)


def unstriped8(offs):
    return offs.reshape(8, 16, -1).transpose(0, 2, 1).reshape(8, -1).astype(np.int64)


def pick8(x, idx, run):
    r = np.arange(len(x))
    return x[r[:, None], idx[r % (8 * run) // run]]


E2M1 = np.array([0.0, 0.5, 1.0, 1.5, 2.0, 3.0, 4.0, 6.0, -0.0, -0.5, -1.0, -1.5, -2.0, -3.0, -4.0, -6.0])


def pack_weight(w, fmt):
    k, n = w.shape
    w = f64(np.asarray(w, np.float32).astype(ml_dtypes.bfloat16)).reshape(k // 32, 32, n)
    amax = np.abs(w).max(1)
    if fmt in ("e4m3", "e5m2"):
        byte = np.frexp(amax)[1] - 1 + 127 - (7 if fmt == "e4m3" else 14)
    else:
        mant, ex = np.frexp(amax / 6.0)
        byte = np.where(mant > 0.5, ex, ex - 1) + 127
    byte = np.clip(np.where(amax > 0, byte, 1), 1, 254)
    scaled = (w * np.exp2(127.0 - byte)[:, None, :]).reshape(k, n).astype(np.float32)
    by_word = np.ascontiguousarray(scaled.reshape(k // 512, 128, 4, n).transpose(0, 1, 3, 2))
    if fmt in ("e4m3", "e5m2"):
        words = by_word.astype(ml_dtypes.float8_e4m3fn if fmt == "e4m3" else ml_dtypes.float8_e5m2).view(np.uint8)
    else:
        c = by_word.astype(ml_dtypes.float4_e2m1fn).view(np.uint8) & 0xF
        words = (c[..., 0::2] | (c[..., 1::2] << 4)).reshape(k // 512, 128, 2 * n)
    return np.ascontiguousarray(words), np.ascontiguousarray(byte.astype(np.uint8).reshape(k // 512, 16, n))


def unpack_weight(words, scales, fmt):
    g, _, n = scales.shape
    words = np.ascontiguousarray(words).reshape(g, 128, n, -1)
    if fmt in ("e4m3", "e5m2"):
        vals = words.view(ml_dtypes.float8_e4m3fn if fmt == "e4m3" else ml_dtypes.float8_e5m2).astype(np.float64)
    else:
        nib = np.empty((g, 128, n, 4), np.uint8)
        nib[..., 0::2] = words & 0xF
        nib[..., 1::2] = words >> 4
        vals = E2M1[nib]
    vals = vals * np.repeat(np.exp2(scales.astype(np.float64) - 127.0), 8, axis=1)[..., None]
    return vals.transpose(0, 1, 3, 2).reshape(g * 512, n)


def sgn(shape):
    return np.random.uniform(0.5, 2.0, shape) * np.where(np.random.standard_normal(shape) < 0, -1.0, 1.0)


K, T, J, R, C, O, N, U, E = 512, 1024, 256, 512, 1024, 256, 256, 128, 512


def setup_inputs():
    n = np.random.standard_normal
    idx = np.random.permutation(T)[:J]
    idx2 = np.random.permutation(J)[:J]
    idx3 = np.stack([np.random.permutation(C)[:J] for _ in range(8)])
    idx4 = np.stack([np.random.permutation(C)[:O] for _ in range(8)])
    idx5 = np.random.permutation(T)[:O]
    idx6 = np.random.permutation(O)[:U]
    idx7 = np.random.permutation(E)[:U]
    fk = mx_kscale(K)
    fr = mx_kscale(R)
    xtp = pack_weight(n((K, T)) / fk[:, None], "e5m2")
    wp = pack_weight(n((K, R)) * 1 / np.sqrt(K) * fk[:, None] * fr, "e2m1")
    w2p = pack_weight(n((K, R)) * 1 / np.sqrt(K) * fk[:, None] * fr, "e4m3")
    wbp = pack_weight(n((R, N)) * 1 / np.sqrt(R) / fr[:, None], "e2m1")
    wsp = pack_weight(n((K, N)) * 1 / np.sqrt(K) * fk[:, None], "e2m1")
    return {
        "xt_words": xtp[0],
        "xt_scales": xtp[1],
        "w_words": wp[0],
        "w_scales": wp[1],
        "w2_words": w2p[0],
        "w2_scales": w2p[1],
        "sa": (sgn((R, 1))).astype(np.float32),
        "wb_words": wbp[0],
        "wb_scales": wbp[1],
        "ws_words": wsp[0],
        "ws_scales": wsp[1],
        "so": (sgn((N, 1))).astype(np.float32),
        "offs": striped(idx),
        "offs2": striped(idx2),
        "offs3": striped8(idx3),
        "offs4": striped8(idx4),
        "offs5": striped(idx5),
        "offs6": striped(idx6),
        "offs7": striped(idx7),
    }


def reference(xt_words, xt_scales, w_words, w_scales, w2_words, w2_scales, sa, wb_words, wb_scales, ws_words, ws_scales, so, offs, offs2, offs3, offs4, offs5, offs6, offs7):
    idx = unstriped(offs)
    idx2 = unstriped(offs2)
    idx3 = unstriped8(offs3)
    idx4 = unstriped8(offs4)
    idx5 = unstriped(offs5)
    idx6 = unstriped(offs6)
    idx7 = unstriped(offs7)
    xtu = unpack_weight(xt_words, xt_scales, "e5m2")
    wu = unpack_weight(w_words, w_scales, "e2m1")
    w2u = unpack_weight(w2_words, w2_scales, "e4m3")
    wbu = unpack_weight(wb_words, wb_scales, "e2m1")
    wsu = unpack_weight(ws_words, ws_scales, "e2m1")
    xtidxg = xtu[:, idx]
    a = wu.T @ xtidxg
    b = w2u.T @ xtidxg
    h1 = np.maximum(a, b[:, idx2] * f64(sa))
    pw = np.zeros((R, C))
    pw[np.arange(R)[:, None], idx3[np.arange(R) % 512 // 64]] = h1
    hid = pick8(pw, idx4, 64)
    hidq = mxq(hid, 0, "e4m3")
    xtidx5g = xtu[:, idx5]
    p = wbu.T @ hidq + wsu.T @ xtidx5g
    m0 = p[:, idx6] * f64(so)
    y = np.zeros((N, E))
    y[:, idx7] = m0
    return y

from contextlib import ExitStack

import concourse.mybir as mybir

K, T, J, R, C, O, N, U, E = 512, 1024, 256, 512, 1024, 256, 256, 128, 512
FLOPS = 2 * K * R * J * 2 + 2 * R * N * O + 2 * K * N * O

F32 = mybir.dt.float32
BF16 = mybir.dt.bfloat16
I32 = mybir.dt.int32
U32 = mybir.dt.uint32
U16 = mybir.dt.uint16
U8 = mybir.dt.uint8
E4M3 = mybir.dt.float8_e4m3fn_x4
E5M2 = mybir.dt.float8_e5m2_x4
E2M1 = mybir.dt.float4_e2m1fn_x4
COPY = mybir.ActivationFunctionType.Copy
MAX = mybir.AluOpType.max

P = 128
PACK = 4
QUADS = 4
HALVES = N // P


def tile_list_ownlater_twow_further_postedout_kernel(
    tc, xt_words, xt_scales, w_words, w_scales, w2_words, w2_scales, sa, wb_words, wb_scales,
    ws_words, ws_scales, so, offs, offs2, offs3, offs4, offs5, offs6, offs7, out,
):
    nc = tc.nc
    with ExitStack() as ctx:
        keep = ctx.enter_context(tc.tile_pool(name="keep", bufs=1))
        reuse = ctx.enter_context(tc.tile_pool(name="reuse", bufs=2))
        wide = ctx.enter_context(tc.tile_pool(name="wide", bufs=4))
        hold = ctx.enter_context(tc.tile_pool(name="hold", bufs=1))
        psum = ctx.enter_context(tc.psum_pool(name="psum", bufs=4))

        def load_list(src, name):
            t = keep.tile([P, src.shape[1]], U16, name=name)
            nc.sync.dma_start(t[:], src)
            return t

        def zero_plane(width, name):
            plane = keep.tile([P, width], U8, name=name, align_bytes=64)
            nc.vector.memset(plane[:].bitcast(I32), 0)
            return plane

        def load_plane(queue, plane, scales):
            rows = scales[0].bitcast(I32)
            for q in range(QUADS):
                queue.dma_start(plane[:].bitcast(I32)[32 * q : 32 * q + 4, :], rows[4 * q : 4 * q + 4, :])

        def load_words(queue, words, nbytes, name):
            t = keep.tile([P, nbytes // 4], I32, name=name, align_bytes=64)
            queue.dma_start(t[:], words.bitcast(I32))
            return t

        def stage_rows(queue, rows, scales):
            queue.dma_start(
                rows[0:4, :].rearrange("r (q n) -> r q n", q=QUADS),
                scales[0].bitcast(I32).rearrange("(q r) n -> r q n", q=QUADS),
            )

        def spread_rows(plane, rows, first):
            for q in range(first, QUADS):
                nc.vector.tensor_copy(
                    plane[32 * q : 32 * q + 4, 0 : R // 4], rows[0:4, q * R // 4 : (q + 1) * R // 4]
                )

        x_plane = zero_plane(T, "x_plane")
        w2_rows = keep.tile([4, QUADS * R // 4], I32, name="w2_rows", align_bytes=64)
        w2_plane = keep.tile([P, R // 4], I32, name="w2_plane", align_bytes=64)
        nc.vector.memset(w2_plane[:], 0)
        w_plane = reuse.tile([P, R], U8, name="w_plane", tag="reuse", align_bytes=64)
        nc.vector.memset(w_plane[:].bitcast(I32), 0)
        ws_plane = zero_plane(N, "ws_plane")
        wb_plane = zero_plane(N, "wb_plane")

        l1 = load_list(offs, "l1")
        load_plane(nc.scalar, x_plane, xt_scales)
        stage_rows(nc.sync, w2_rows, w2_scales)
        x_raw = load_words(nc.sync, xt_words[0].rearrange("p c r -> p (c r)"), 4 * T, "x_raw")
        w2_raw = load_words(nc.sync, w2_words[0].rearrange("p c r -> p (c r)"), 4 * R, "w2_raw")
        l2 = load_list(offs2, "l2")
        sa_sb = keep.tile([P, PACK], F32, name="sa_sb")
        nc.gpsimd.dma_start(sa_sb[:], sa.rearrange("(p t) one -> p (t one)", t=PACK))
        w_raw = reuse.tile([P, R // 2], I32, name="w_raw", tag="reuse", align_bytes=64)
        nc.sync.dma_start(w_raw[:], w_words[0].bitcast(I32))
        load_plane(nc.sync, w_plane, w_scales)
        l3 = load_list(offs3, "l3")
        l5 = load_list(offs5, "l5")
        l4 = load_list(offs4, "l4")
        ws_sb = load_words(nc.sync, ws_words[0], 2 * N, "ws_sb")
        load_plane(nc.sync, ws_plane, ws_scales)
        wb_sb = load_words(nc.sync, wb_words[0], 2 * N, "wb_sb")
        load_plane(nc.sync, wb_plane, wb_scales)
        so_sb = keep.tile([P, HALVES], F32, name="so_sb")
        with nc.allow_non_contiguous_dma(reason="one weight a partition"):
            nc.sync.dma_start(so_sb[:], so.rearrange("(h p) one -> p (h one)", p=P))
        l6 = load_list(offs6, "l6")
        l7 = load_list(offs7, "l7")

        def gather_tokens(lst, name, scale_tag, words_tag):
            scale = hold.tile([P, J], U8, name=name + "_scale", tag=scale_tag, align_bytes=64)
            words = hold.tile([P, J], U32, name=name + "_words", tag=words_tag, align_bytes=64)
            nc.vector.tensor_copy(scale[:], x_plane[:].indirect(lst[:]))
            nc.vector.tensor_copy(words[:], x_raw[:].bitcast(U32).indirect(lst[:]))
            return words, scale

        spread_rows(w2_plane, w2_rows, 0)

        w2_first = hold.tile([P, P], U32, name="w2_first", tag="first_words", align_bytes=64)
        w2_rest = keep.tile([P, PACK - 1, P], U32, name="w2_rest", align_bytes=64)
        w2_first_scale = hold.tile([P, P], U8, name="w2_first_scale", tag="first_scale", align_bytes=64)
        w2_rest_scale = keep.tile([P, PACK - 1, P], U8, name="w2_rest_scale", align_bytes=64)
        w2_plane_tm = w2_plane[:].bitcast(U8).rearrange("p (m t) -> p t m", t=PACK)
        nc.vector.tensor_copy(w2_first_scale[:], w2_plane_tm[:, 0, :])
        xg, xg_scale = gather_tokens(l1, "xg", "xg_scale", "xg_words")
        nc.vector.tensor_copy(w2_rest_scale[:], w2_plane_tm[:, 1:PACK, :])
        w2_tm = w2_raw[:].bitcast(U32).rearrange("p (m t) -> p t m", t=PACK)
        nc.scalar.copy(w2_first[:], w2_tm[:, 0, :])
        nc.scalar.copy(
            w2_rest[:].rearrange("p t (c i) -> p c t i", i=4),
            w2_tm[:, 1:PACK, :].rearrange("p t (c i) -> p c t i", i=4),
        )

        b_ps = []
        for t in range(PACK):
            bank = psum.tile([P, J], F32, name="b_bank", tag="early")
            words = w2_first[:] if t == 0 else w2_rest[:, t - 1, :]
            scale = w2_first_scale[:] if t == 0 else w2_rest_scale[:, t - 1, :]
            nc.tensor.matmul_mx(
                out=bank[:], lhsT=words.bitcast(E4M3), lhsT_scale=scale,
                rhs=xg[:].bitcast(E5M2), rhs_scale=xg_scale[:], start=True, stop=True,
            )
            b_ps.append(bank)

        partner = []
        for t in range(PACK):
            b_sb = wide.tile([P, 2 * J], F32, name="b_sb", tag="wide")
            if t == 0:
                nc.scalar.activation(b_sb[:, 0:J], b_ps[t][:], COPY)
            else:
                nc.vector.tensor_copy(b_sb[:, 0:J], b_ps[t][:])
            prod = hold.tile([P, J], F32, name="partner", tag="partner%d" % t, align_bytes=64)
            nc.scalar.activation(prod[:], b_sb[:].indirect(l2[:]), COPY, scale=sa_sb[:, t : t + 1])
            partner.append(prod)

        w_first = hold.tile([P, P], U16, name="w_first", tag="first_words", align_bytes=64)
        w_first_scale = hold.tile([P, P], U8, name="w_first_scale", tag="first_scale", align_bytes=64)
        w_tm = w_raw[:].bitcast(U16).rearrange("p (m t) -> p t m", t=PACK)
        w_plane_tm = w_plane[:].rearrange("p (m t) -> p t m", t=PACK)
        nc.vector.tensor_copy(w_first[:], w_tm[:, 0, :])
        nc.vector.tensor_copy(w_first_scale[:], w_plane_tm[:, 0, :])

        h1 = []
        for t in range(PACK):
            if t == 1:
                w_rest = hold.tile([P, PACK - 1, P], U16, name="w_rest", tag="first_words", align_bytes=64)
                w_rest_scale = hold.tile([P, PACK - 1, P], U8, name="w_rest_scale", tag="first_scale", align_bytes=64)
                nc.vector.tensor_copy(w_rest[:], w_tm[:, 1:PACK, :])
                nc.vector.tensor_copy(w_rest_scale[:], w_plane_tm[:, 1:PACK, :])
            bank = psum.tile([P, J], F32, name="a_bank", tag="late")
            words = w_first[:] if t == 0 else w_rest[:, t - 1, :]
            scale = w_first_scale[:] if t == 0 else w_rest_scale[:, t - 1, :]
            nc.tensor.matmul_mx(
                out=bank[:], lhsT=words.bitcast(E2M1), lhsT_scale=scale,
                rhs=xg[:].bitcast(E5M2), rhs_scale=xg_scale[:], start=True, stop=True,
            )
            kept = keep.tile([P, J], F32, name="h1_%d" % t)
            nc.vector.tensor_tensor(kept[:], bank[:], partner[t][:], MAX)
            h1.append(kept)

        xs, xs_scale = gather_tokens(l5, "xs", "partner2", "partner3")
        parts = [slice(0, O // 2), slice(O // 2, O)]
        p_ps = {}
        for i, cols in enumerate(parts):
            for h in range(HALVES):
                bank = psum.tile([P, O // 2], F32, name="p_bank", tag="early")
                nc.tensor.matmul_mx(
                    out=bank[:], lhsT=ws_sb[:].bitcast(U16)[:, h * P : (h + 1) * P].bitcast(E2M1),
                    lhsT_scale=ws_plane[:, h * P : (h + 1) * P],
                    rhs=xs[:, cols].bitcast(E5M2), rhs_scale=xs_scale[:, cols], start=True, stop=False,
                )
                p_ps[i, h] = bank

        hid = keep.tile([P, PACK, O], F32, name="hid")
        hid_bf = keep.tile([P, O, PACK], BF16, name="hid_bf", align_bytes=64)
        for t in range(PACK):
            if t == 0:
                board = keep.tile([P, C], F32, name="board%d" % t)
                nc.vector.memset(board[:], 0.0)
            else:
                board = wide.tile([P, C], F32, name="board", tag="wide")
                nc.gpsimd.memset(board[:], 0.0)
            nc.scalar.activation(board[:].indirect(l3[:]), h1[t][:], COPY)
            nc.vector.tensor_copy(hid[:, t, :], board[:].indirect(l4[:]))
            if t == PACK - 2:
                nc.vector.tensor_copy(hid_bf[:, :, 0 : PACK - 1], hid[:, 0 : PACK - 1, :].rearrange("p t o -> p o t"))
        pages = []
        for h in range(HALVES):
            page = reuse.tile([P, E], F32, name="page", tag="reuse", align_bytes=64)
            nc.gpsimd.memset(page[:], 0.0)
            pages.append(page)

        hq = keep.tile([P, O], U32, name="hq", align_bytes=64)
        hq_scale = keep.tile([P, O], U8, name="hq_scale", align_bytes=64)
        for cols in parts:
            nc.vector.tensor_copy(hid_bf[:, cols, PACK - 1], hid[:, PACK - 1, cols])
        for cols in parts:
            nc.vector.quantize_mx(
                out=hq[:, cols].bitcast(E4M3), scales=hq_scale[:, cols],
                in_=hid_bf[:, cols, :].rearrange("p o t -> p (o t)"),
            )
        for i, cols in enumerate(parts):
            for h in range(HALVES):
                nc.tensor.matmul_mx(
                    out=p_ps[i, h][:], lhsT=wb_sb[:].bitcast(U16)[:, h * P : (h + 1) * P].bitcast(E2M1),
                    lhsT_scale=wb_plane[:, h * P : (h + 1) * P],
                    rhs=hq[:, cols].bitcast(E4M3), rhs_scale=hq_scale[:, cols], start=False, stop=True,
                )
        ends = []
        for h in range(HALVES):
            p_sb = keep.tile([P, O], F32, name="p_sb%d" % h)
            for i, cols in enumerate(parts):
                if h == 0:
                    nc.scalar.activation(p_sb[:, cols], p_ps[i, h][:], COPY)
                else:
                    nc.vector.tensor_copy(p_sb[:, cols], p_ps[i, h][:])
            m0 = keep.tile([P, U], F32, name="m0_%d" % h)
            nc.scalar.activation(m0[:], p_sb[:].indirect(l6[:]), COPY, scale=so_sb[:, h : h + 1])
            ends.append(m0)
        nc.vector.tensor_copy(pages[0][:].indirect(l7[:]), ends[0][:])
        nc.sync.dma_start(out[0:P, :], pages[0][:])
        nc.scalar.activation(pages[1][:].indirect(l7[:]), ends[1][:], COPY)
        nc.scalar.dma_start(out[P : 2 * P, :], pages[1][:])
